import numpy as np
CORES = [7,14,21,28,35,42,49,56,71,78,85,92,99,106,113,120]
N = 16
def setup_inputs(rng):
    return {"x1": rng.standard_normal((N, 128, 256), dtype=np.float32), "x2": rng.standard_normal((N, 128, 1), dtype=np.float32), "x3": rng.standard_normal((N, 128, 1024), dtype=np.float32), "x4": rng.standard_normal((N, 128, 64), dtype=np.float32)}
def reference(x1, x2, x3, x4):
    out = {}
    s = x1.sum(axis=0, dtype=np.float64).astype(x1.dtype)
    out["y1"] = np.broadcast_to(s, (N,) + s.shape)
    s = x2.sum(axis=0, dtype=np.float64).astype(x2.dtype)
    out["y2"] = np.broadcast_to(s, (N,) + s.shape)
    s = x3.sum(axis=0, dtype=np.float64).astype(x3.dtype)
    out["y3"] = np.broadcast_to(s, (N,) + s.shape)
    s = x4.sum(axis=0, dtype=np.float64).astype(x4.dtype)
    out["y4"] = np.broadcast_to(s, (N,) + s.shape)
    return out

@@ -1,0 +1,67 @@
+from concourse.bass import DstId, RemoteDMATransfer
+
+W = 1345
+PW = 169
+BOUNDS = [168 * j for j in range(8)] + [W]
+
+SCRATCH = {
+    "pack": ("sbuf", [128, W], "float32"),
+    "res": ("sbuf", [128, W], "float32"),
+    "slot": ("sbuf", [128, 9 * PW], "float32"),
+}
+SEMAPHORES = ["loaded", "sent", "arrived", "mate", "done", "stored"]
+
+COLS = {"1": (1024, 1280), "2": (1344, 1345), "3": (0, 1024), "4": (1280, 1344)}
+
+
+def owner_of(T, chip):
+    local = T.cores[chip] % 8
+    return chip * 8 + (3 if local >= 4 else 7)
+
+
+def rank_program(g, core, T, topo):
+    chip = topo.chip(core)
+    plane = chip & 1
+    rank = T.rank_of(core)
+    if rank is not None:
+        qs = {"1": g.scalar, "2": g.scalar, "3": g.sync, "4": g.scalar}
+        for k, (a, b) in COLS.items():
+            qs[k].dma_start(T.pack[:, a:b], T["x" + k][:]).then_inc(T.sem.loaded, 16)
+        g.wait_ge(T.sem.loaded, 64)
+        me = chip // 2
+        sent = 0
+        for j in range(8):
+            a, b = BOUNDS[j], BOUNDS[j + 1]
+            dst = owner_of(T, 2 * j + plane)
+            rid, pid, _se = topo.addr(dst)
+            g.remote_dma(T.slot[:, me * PW:me * PW + (b - a)], T.pack[:, a:b], T.sem.arrived, T.sem.sent,
+                         pid, rid, 0xFF)
+            sent += 8
+        g.wait_ge(T.sem.sent, sent)
+        g.wait_ge(T.sem.done, 64)
+        g.sync.wait_ge(T.sem.done, 64)
+        g.scalar.wait_ge(T.sem.done, 64)
+        for k, (a, b) in COLS.items():
+            qs[k].dma_start(T["y" + k][:], T.res[:, a:b]).then_inc(T.sem.stored, 16)
+        g.wait_ge(T.sem.stored, 64)
+        return
+    if core != owner_of(T, chip):
+        return
+    j = chip // 2
+    a, b = BOUNDS[j], BOUNDS[j + 1]
+    w = b - a
+    srcs = [T.slot[:, s * PW:s * PW + w] for s in range(9)]
+    g.wait_ge(T.sem.arrived, 64)
+    rid, pid, _se = topo.addr(owner_of(T, chip ^ 1))
+    g.remote_dma_fused([RemoteDMATransfer(dst_ids=[DstId(rid=rid, pnc=pid)], dma_engine_mask=0xFF,
+                                          remote_sem=T.sem.mate, srcs=srcs[:8], dsts=[srcs[8]], alu_op=1)],
+                       local_sem=T.sem.sent)
+    g.wait_ge(T.sem.mate, 8)
+    ids = []
+    for i in range(8):
+        rid, pid, _se = topo.addr(T.cores[2 * i + plane])
+        ids.append(DstId(rid=rid, pnc=pid))
+    g.remote_dma_fused([RemoteDMATransfer(dst_ids=ids, dma_engine_mask=0xFF, remote_sem=T.sem.done,
+                                          srcs=srcs, dsts=[T.res[:, a:b]] * 8, alu_op=1)],
+                       local_sem=T.sem.sent)
+    g.wait_ge(T.sem.sent, 16)

@@ -1,67 +1,101 @@
 from concourse.bass import DstId, RemoteDMATransfer
 
-W = 1345
-PW = 169
-BOUNDS = [168 * j for j in range(8)] + [W]
+PARTS = [("A", k, 168, k, 0) for k in range(6)] + [
+    ("B", None, 32, 6, 0), ("C", None, 136, 6, 1), ("D", None, 49, 7, 0), ("E", None, 120, 7, 1)]
+SMALL = PARTS[6:]
 
 SCRATCH = {
-    "pack": ("sbuf", [128, W], "float32"),
-    "res": ("sbuf", [128, W], "float32"),
-    "slot": ("sbuf", [128, 9 * PW], "float32"),
+    "pA": ("dram", [6, 128, 168], "float32"), "rA": ("dram", [6, 128, 168], "float32"),
+    "sA": ("dram", [9, 128, 168], "float32"),
 }
-SEMAPHORES = ["loaded", "sent", "arrived", "mate", "done", "stored"]
+for _l, _k, _n, _p, _h in SMALL:
+    SCRATCH["p" + _l] = ("dram", [128, _n], "float32")
+    SCRATCH["r" + _l] = ("dram", [128, _n], "float32")
+    SCRATCH["s" + _l] = ("dram", [9, 128, _n], "float32")
 
-COLS = {"1": (1024, 1280), "2": (1344, 1345), "3": (0, 1024), "4": (1280, 1344)}
-
-
-def owner_of(T, chip):
-    local = T.cores[chip] % 8
-    return chip * 8 + (3 if local >= 4 else 7)
+SEMAPHORES = ["ld_big", "ld_small", "sent", "arrived", "mate", "done_big", "done_small", "stored"]
 
 
-def rank_program(g, core, T, topo):
+def sections(T, pre, io):
+    t1, t2, t3, t4 = T[io + "1"], T[io + "2"], T[io + "3"], T[io + "4"]
+    big = (T[pre + "A"][:], t3[0:126, :])
+    small = [
+        (T[pre + "E"][:], t1[0:60, :]),
+        (T[pre + "C"][:], t1[60:128, :]),
+        (T[pre + "D"][:], t4[30:128, :]),
+        (T[pre + "B"][0:64, :], t3[126:128, :]),
+        (T[pre + "B"][68:128, :], t4[0:30, :]),
+        (T[pre + "B"][64:68, :], t2[:]),
+    ]
+    return big, small
+
+
+def owner(T, chip, which):
+    return chip * 8 + (2 if T.cores[chip] % 8 >= 4 else 6) + which
+
+
+def engines(mask):
+    return bin(mask).count("1")
+
+
+def rank_side(g, core, T, topo):
+    chip = topo.chip(core)
+    plane, me = chip & 1, chip // 2
+    big, small = sections(T, "p", "x")
+    g.sync.dma_start(big[0], big[1]).then_inc(T.sem.ld_big, 16)
+    for i, (b, x) in enumerate(small):
+        (g.scalar if i % 2 == 0 else g.sync).dma_start(b, x).then_inc(T.sem.ld_small, 16)
+    sent = 0
+    g.wait_ge(T.sem.ld_small, 16 * len(small))
+    order = SMALL + [PARTS[(me + 1 + k) % 6] for k in range(6)]
+    for i, (l, k, n, piece, which) in enumerate(order):
+        if i == len(SMALL):
+            g.wait_ge(T.sem.ld_big, 16)
+        dst = owner(T, 2 * piece + plane, which)
+        rid, pid, _se = topo.addr(dst)
+        m = topo.mask(core, dst)
+        src = T["p" + l][:] if k is None else T["p" + l][k]
+        g.remote_dma(T["s" + l][me], src, T.sem.arrived, T.sem.sent, pid, rid, m)
+        sent += engines(m)
+    g.wait_ge(T.sem.sent, sent)
+    big, small = sections(T, "r", "y")
+    g.sync.wait_ge(T.sem.done_small, 8 * len(SMALL))
+    g.scalar.wait_ge(T.sem.done_small, 8 * len(SMALL))
+    for i, (b, y) in enumerate(small):
+        (g.scalar if i % 2 == 0 else g.sync).dma_start(y, b).then_inc(T.sem.stored, 16)
+    g.scalar.wait_ge(T.sem.done_big, 8 * 6)
+    g.scalar.dma_start(big[1], big[0]).then_inc(T.sem.stored, 16)
+    g.wait_ge(T.sem.stored, 16 * (len(small) + 1))
+
+
+def owner_side(g, core, T, topo, part):
+    l, k, n, piece, which = part
     chip = topo.chip(core)
     plane = chip & 1
-    rank = T.rank_of(core)
-    if rank is not None:
-        qs = {"1": g.scalar, "2": g.scalar, "3": g.sync, "4": g.scalar}
-        for k, (a, b) in COLS.items():
-            qs[k].dma_start(T.pack[:, a:b], T["x" + k][:]).then_inc(T.sem.loaded, 16)
-        g.wait_ge(T.sem.loaded, 64)
-        me = chip // 2
-        sent = 0
-        for j in range(8):
-            a, b = BOUNDS[j], BOUNDS[j + 1]
-            dst = owner_of(T, 2 * j + plane)
-            rid, pid, _se = topo.addr(dst)
-            g.remote_dma(T.slot[:, me * PW:me * PW + (b - a)], T.pack[:, a:b], T.sem.arrived, T.sem.sent,
-                         pid, rid, 0xFF)
-            sent += 8
-        g.wait_ge(T.sem.sent, sent)
-        g.wait_ge(T.sem.done, 64)
-        g.sync.wait_ge(T.sem.done, 64)
-        g.scalar.wait_ge(T.sem.done, 64)
-        for k, (a, b) in COLS.items():
-            qs[k].dma_start(T["y" + k][:], T.res[:, a:b]).then_inc(T.sem.stored, 16)
-        g.wait_ge(T.sem.stored, 64)
-        return
-    if core != owner_of(T, chip):
-        return
-    j = chip // 2
-    a, b = BOUNDS[j], BOUNDS[j + 1]
-    w = b - a
-    srcs = [T.slot[:, s * PW:s * PW + w] for s in range(9)]
-    g.wait_ge(T.sem.arrived, 64)
-    rid, pid, _se = topo.addr(owner_of(T, chip ^ 1))
+    slots = [T["s" + l][s] for s in range(9)]
+    g.wait_ge(T.sem.arrived, 7 * 8 + 16)
+    rid, pid, _se = topo.addr(owner(T, chip ^ 1, which))
     g.remote_dma_fused([RemoteDMATransfer(dst_ids=[DstId(rid=rid, pnc=pid)], dma_engine_mask=0xFF,
-                                          remote_sem=T.sem.mate, srcs=srcs[:8], dsts=[srcs[8]], alu_op=1)],
+                                          remote_sem=T.sem.mate, srcs=slots[:8], dsts=[slots[8]], alu_op=1)],
                        local_sem=T.sem.sent)
     g.wait_ge(T.sem.mate, 8)
     ids = []
     for i in range(8):
         rid, pid, _se = topo.addr(T.cores[2 * i + plane])
         ids.append(DstId(rid=rid, pnc=pid))
-    g.remote_dma_fused([RemoteDMATransfer(dst_ids=ids, dma_engine_mask=0xFF, remote_sem=T.sem.done,
-                                          srcs=srcs, dsts=[T.res[:, a:b]] * 8, alu_op=1)],
+    out = T["r" + l][:] if k is None else T["r" + l][k]
+    g.remote_dma_fused([RemoteDMATransfer(dst_ids=ids, dma_engine_mask=0xFF,
+                                          remote_sem=T.sem.done_small if k is None else T.sem.done_big,
+                                          srcs=slots, dsts=[out] * 8, alu_op=1)],
                        local_sem=T.sem.sent)
     g.wait_ge(T.sem.sent, 16)
+
+
+def rank_program(g, core, T, topo):
+    if T.rank_of(core) is not None:
+        rank_side(g, core, T, topo)
+        return
+    chip = topo.chip(core)
+    for part in PARTS:
+        if part[3] == chip // 2 and core == owner(T, chip, part[4]):
+            owner_side(g, core, T, topo, part)

@@ -13,7 +13,7 @@ for _l, _k, _n, _p, _h in SMALL:
     SCRATCH["r" + _l] = ("dram", [128, _n], "float32")
     SCRATCH["s" + _l] = ("dram", [9, 128, _n], "float32")
 
-SEMAPHORES = ["ld_big", "ld_small", "sent", "arrived", "mate", "done_big", "done_small", "stored"]
+SEMAPHORES = ["ld_big", "ld_small", "sent", "arrived", "mate", "done_big", "done_small", "stored", "st_big"]
 
 
 def sections(T, pre, io):
@@ -42,30 +42,35 @@ def rank_side(g, core, T, topo):
     chip = topo.chip(core)
     plane, me = chip & 1, chip // 2
     big, small = sections(T, "p", "x")
-    g.sync.dma_start(big[0], big[1]).then_inc(T.sem.ld_big, 16)
+    g.dma_start(big[0], big[1]).then_inc(T.sem.ld_big, 16)
     for i, (b, x) in enumerate(small):
         (g.scalar if i % 2 == 0 else g.sync).dma_start(b, x).then_inc(T.sem.ld_small, 16)
     sent = 0
-    g.wait_ge(T.sem.ld_small, 16 * len(small))
-    order = SMALL + [PARTS[(me + 1 + k) % 6] for k in range(6)]
-    for i, (l, k, n, piece, which) in enumerate(order):
-        if i == len(SMALL):
-            g.wait_ge(T.sem.ld_big, 16)
-        dst = owner(T, 2 * piece + plane, which)
-        rid, pid, _se = topo.addr(dst)
-        m = topo.mask(core, dst)
-        src = T["p" + l][:] if k is None else T["p" + l][k]
-        g.remote_dma(T["s" + l][me], src, T.sem.arrived, T.sem.sent, pid, rid, m)
-        sent += engines(m)
+    waited = set()
+    for t in range(8):
+        for l, k, n, piece, which in PARTS:
+            if piece != (me + 1 + t) % 8:
+                continue
+            need = ("ld_small", 16 * len(small)) if k is None else ("ld_big", 16)
+            if need[0] not in waited:
+                g.wait_ge(T.sem[need[0]], need[1])
+                waited.add(need[0])
+            dst = owner(T, 2 * piece + plane, which)
+            rid, pid, _se = topo.addr(dst)
+            m = topo.mask(core, dst)
+            src = T["p" + l][:] if k is None else T["p" + l][k]
+            g.remote_dma(T["s" + l][me], src, T.sem.arrived, T.sem.sent, pid, rid, m)
+            sent += engines(m)
     g.wait_ge(T.sem.sent, sent)
     big, small = sections(T, "r", "y")
     g.sync.wait_ge(T.sem.done_small, 8 * len(SMALL))
     g.scalar.wait_ge(T.sem.done_small, 8 * len(SMALL))
     for i, (b, y) in enumerate(small):
         (g.scalar if i % 2 == 0 else g.sync).dma_start(y, b).then_inc(T.sem.stored, 16)
-    g.scalar.wait_ge(T.sem.done_big, 8 * 6)
-    g.scalar.dma_start(big[1], big[0]).then_inc(T.sem.stored, 16)
-    g.wait_ge(T.sem.stored, 16 * (len(small) + 1))
+    g.wait_ge(T.sem.done_big, 8 * 6)
+    g.dma_start(big[1], big[0]).then_inc(T.sem.st_big, 16)
+    g.wait_ge(T.sem.st_big, 16)
+    g.wait_ge(T.sem.stored, 16 * len(small))
 
 
 def owner_side(g, core, T, topo, part):

from concourse.bass import DstId, RemoteDMATransfer

PARTS = [("A", k, 168, k, 0) for k in range(6)] + [
    ("B", None, 32, 6, 0), ("C", None, 136, 6, 1), ("D", None, 49, 7, 0), ("E", None, 120, 7, 1)]
SMALL = PARTS[6:]

SCRATCH = {
    "pA": ("dram", [6, 128, 168], "float32"), "rA": ("dram", [6, 128, 168], "float32"),
    "sA": ("dram", [9, 128, 168], "float32"),
}
for _l, _k, _n, _p, _h in SMALL:
    SCRATCH["p" + _l] = ("dram", [128, _n], "float32")
    SCRATCH["r" + _l] = ("dram", [128, _n], "float32")
    SCRATCH["s" + _l] = ("dram", [9, 128, _n], "float32")

SEMAPHORES = ["ld_big", "ld_small", "sent", "arrived", "mate", "done_big", "done_small", "stored", "st_big"]


def sections(T, pre, io):
    t1, t2, t3, t4 = T[io + "1"], T[io + "2"], T[io + "3"], T[io + "4"]
    big = (T[pre + "A"][:], t3[0:126, :])
    small = [
        (T[pre + "E"][:], t1[0:60, :]),
        (T[pre + "C"][:], t1[60:128, :]),
        (T[pre + "D"][:], t4[30:128, :]),
        (T[pre + "B"][0:64, :], t3[126:128, :]),
        (T[pre + "B"][68:128, :], t4[0:30, :]),
        (T[pre + "B"][64:68, :], t2[:]),
    ]
    return big, small


def owner(T, chip, which):
    return chip * 8 + (2 if T.cores[chip] % 8 >= 4 else 6) + which


def engines(mask):
    return bin(mask).count("1")


def rank_side(g, core, T, topo):
    chip = topo.chip(core)
    plane, me = chip & 1, chip // 2
    big, small = sections(T, "p", "x")
    g.dma_start(big[0], big[1]).then_inc(T.sem.ld_big, 16)
    for i, (b, x) in enumerate(small):
        (g.scalar if i % 2 == 0 else g.sync).dma_start(b, x).then_inc(T.sem.ld_small, 16)
    sent = 0
    waited = set()
    for t in range(8):
        for l, k, n, piece, which in PARTS:
            if piece != (me + 1 + t) % 8:
                continue
            need = ("ld_small", 16 * len(small)) if k is None else ("ld_big", 16)
            if need[0] not in waited:
                g.wait_ge(T.sem[need[0]], need[1])
                waited.add(need[0])
            dst = owner(T, 2 * piece + plane, which)
            rid, pid, _se = topo.addr(dst)
            m = topo.mask(core, dst)
            src = T["p" + l][:] if k is None else T["p" + l][k]
            g.remote_dma(T["s" + l][me], src, T.sem.arrived, T.sem.sent, pid, rid, m)
            sent += engines(m)
    g.wait_ge(T.sem.sent, sent)
    big, small = sections(T, "r", "y")
    g.sync.wait_ge(T.sem.done_small, 8 * len(SMALL))
    g.scalar.wait_ge(T.sem.done_small, 8 * len(SMALL))
    for i, (b, y) in enumerate(small):
        (g.scalar if i % 2 == 0 else g.sync).dma_start(y, b).then_inc(T.sem.stored, 16)
    g.wait_ge(T.sem.done_big, 8 * 6)
    g.dma_start(big[1], big[0]).then_inc(T.sem.st_big, 16)
    g.wait_ge(T.sem.st_big, 16)
    g.wait_ge(T.sem.stored, 16 * len(small))


def owner_side(g, core, T, topo, part):
    l, k, n, piece, which = part
    chip = topo.chip(core)
    plane = chip & 1
    slots = [T["s" + l][s] for s in range(9)]
    g.wait_ge(T.sem.arrived, 7 * 8 + 16)
    rid, pid, _se = topo.addr(owner(T, chip ^ 1, which))
    g.remote_dma_fused([RemoteDMATransfer(dst_ids=[DstId(rid=rid, pnc=pid)], dma_engine_mask=0xFF,
                                          remote_sem=T.sem.mate, srcs=slots[:8], dsts=[slots[8]], alu_op=1)],
                       local_sem=T.sem.sent)
    g.wait_ge(T.sem.mate, 8)
    ids = []
    for i in range(8):
        rid, pid, _se = topo.addr(T.cores[2 * i + plane])
        ids.append(DstId(rid=rid, pnc=pid))
    out = T["r" + l][:] if k is None else T["r" + l][k]
    g.remote_dma_fused([RemoteDMATransfer(dst_ids=ids, dma_engine_mask=0xFF,
                                          remote_sem=T.sem.done_small if k is None else T.sem.done_big,
                                          srcs=slots, dsts=[out] * 8, alu_op=1)],
                       local_sem=T.sem.sent)
    g.wait_ge(T.sem.sent, 16)


def rank_program(g, core, T, topo):
    if T.rank_of(core) is not None:
        rank_side(g, core, T, topo)
        return
    chip = topo.chip(core)
    for part in PARTS:
        if part[3] == chip // 2 and core == owner(T, chip, part[4]):
            owner_side(g, core, T, topo, part)
